import numpy as np
import ml_dtypes


def mxq(x, axis, fmt="e4m3"):
    dtype, down = {"e4m3": (ml_dtypes.float8_e4m3fn, 7), "e5m2": (ml_dtypes.float8_e5m2, 14)}[fmt]
    v = np.moveaxis(np.asarray(x, np.float32).astype(ml_dtypes.bfloat16).astype(np.float64), axis, -1)
    blocks = v.reshape(v.shape[:-1] + (-1, 32))
    amax = np.abs(blocks).max(-1, keepdims=True)
    byte = np.maximum(np.where(amax > 0, np.frexp(amax)[1] - 1 + 127, 0) - down, 1)
    scale = np.exp2(byte - 127.0)
    codes = (blocks / scale).astype(np.float32).astype(dtype).astype(np.float64)
    return np.moveaxis((codes * scale).reshape(v.shape), -1, axis)


WIDE = False


def mx_kscale(k):
    if not WIDE:
        return np.ones(k)
    levels = np.array([10, -10, 5, -5, 0])
    if k % 512:
        return np.exp2(np.random.permutation(np.resize(levels, k // 32))).repeat(32)
    a = np.empty((k // 512, 16))
    for p in range(k // 512):
        a[p, :8] = np.random.permutation(np.resize(levels, 8))
        for g in range(8):
            far = levels[np.abs(levels - a[p, g]) >= 10]
            a[p, g + 8] = far[np.random.randint(len(far))]
    return np.exp2(a.ravel()).repeat(32)


def f64(x):
    return np.asarray(x).astype(np.float64)


def striped(idx):
    return np.tile(np.asarray(idx).reshape(-1, 16).T, (8, 1)).astype(np.uint16)


def unstriped(offs):
    return offs[:16].T.reshape(-1).astype(np.int64)


E2M1 = np.array([0.0, 0.5, 1.0, 1.5, 2.0, 3.0, 4.0, 6.0, -0.0, -0.5, -1.0, -1.5, -2.0, -3.0, -4.0, -6.0])


def pack_weight(w, fmt):
    k, n = w.shape
    w = f64(np.asarray(w, np.float32).astype(ml_dtypes.bfloat16)).reshape(k // 32, 32, n)
    amax = np.abs(w).max(1)
    if fmt == "e4m3":
        byte = np.frexp(amax)[1] - 1 + 127 - 7
    else:
        mant, ex = np.frexp(amax / 6.0)
        byte = np.where(mant > 0.5, ex, ex - 1) + 127
    byte = np.clip(np.where(amax > 0, byte, 1), 1, 254)
    scaled = (w * np.exp2(127.0 - byte)[:, None, :]).reshape(k, n).astype(np.float32)
    by_word = np.ascontiguousarray(scaled.reshape(k // 512, 128, 4, n).transpose(0, 1, 3, 2))
    if fmt == "e4m3":
        words = by_word.astype(ml_dtypes.float8_e4m3fn).view(np.uint8)
    else:
        c = by_word.astype(ml_dtypes.float4_e2m1fn).view(np.uint8) & 0xF
        words = (c[..., 0::2] | (c[..., 1::2] << 4)).reshape(k // 512, 128, 2 * n)
    return np.ascontiguousarray(words), np.ascontiguousarray(byte.astype(np.uint8).reshape(k // 512, 16, n))


def unpack_weight(words, scales, fmt):
    g, _, n = scales.shape
    words = np.ascontiguousarray(words).reshape(g, 128, n, -1)
    if fmt == "e4m3":
        vals = words.view(ml_dtypes.float8_e4m3fn).astype(np.float64)
    else:
        nib = np.empty((g, 128, n, 4), np.uint8)
        nib[..., 0::2] = words & 0xF
        nib[..., 1::2] = words >> 4
        vals = E2M1[nib]
    vals = vals * np.repeat(np.exp2(scales.astype(np.float64) - 127.0), 8, axis=1)[..., None]
    return vals.transpose(0, 1, 3, 2).reshape(g * 512, n)


D, T, I, Q, J, G, M = 512, 2048, 512, 128, 512, 64, 512


def setup_inputs():
    n = np.random.standard_normal
    idx = np.random.permutation(T)[:I]
    idx2 = np.random.permutation(T)[:J]
    idx3 = np.random.permutation(M)[:G]
    fd = mx_kscale(D)
    fj = mx_kscale(J)
    keysp = pack_weight(n((D, T)) / fd[:, None], "e4m3")
    return {
        "query": (n((D, Q)) * 0.6 / np.sqrt(D) * fd[:, None]).astype(np.float32),
        "keys_words": keysp[0],
        "keys_scales": keysp[1],
        "hf": (np.random.uniform(0.5, 2.0, (J, 1)) * fj[:, None]).astype(np.float32),
        "mixer": (n((J, I)) * 0.05 / fj[:, None]).astype(np.float32),
        "lean": (np.random.uniform(0.2, 0.6, (Q, 1))).astype(np.float32),
        "worth": np.tile(np.random.uniform(0.2, 2.0, T), (128, 1)).astype(np.float32),
        "old": (1.0 * n((Q, M))).astype(np.float32),
        "offs": striped(idx),
        "offs2": striped(idx2),
        "offs3": striped(idx3),
    }


def reference(query, keys_words, keys_scales, hf, mixer, lean, worth, old, offs, offs2, offs3):
    idx = unstriped(offs)
    idx2 = unstriped(offs2)
    idx3 = unstriped(offs3)
    keysu = unpack_weight(keys_words, keys_scales, "e4m3")
    keysidx2g = keysu[:, idx2]
    queryq = mxq(f64(query), 0, "e4m3")
    a0 = keysidx2g.T @ queryq
    af = a0 * f64(hf)
    afq = mxq(af, 0, "e4m3")
    mixerq = mxq(f64(mixer), 0, "e4m3")
    mx0 = afq.T @ mixerq
    keysidxg = keysu[:, idx]
    a = queryq.T @ keysidxg
    s = a + mx0
    p = np.exp(s - np.max(s, axis=1, keepdims=True))
    r = p / np.sum(p, axis=1, keepdims=True)
    m0 = np.sum(r * s, axis=1, keepdims=True)
    w = r * ((s - m0) * f64(lean) + 1.0)
    ws = w * f64(worth)[:1][:, idx] * 256.0
    wp = ws.reshape(Q, G, I // G).sum(axis=2)
    wf = np.zeros((Q, M))
    wf[:, idx3] = wp
    y = f64(old) + wf
    return y

@@ -1,0 +1,185 @@
+from contextlib import ExitStack
+
+import concourse.mybir as mybir
+
+F32 = mybir.dt.float32
+BF16 = mybir.dt.bfloat16
+I32 = mybir.dt.int32
+U32 = mybir.dt.uint32
+U16 = mybir.dt.uint16
+U8 = mybir.dt.uint8
+FP8X4 = mybir.dt.float8_e4m3fn_x4
+ALU = mybir.AluOpType
+ACT = mybir.ActivationFunctionType
+AXIS = mybir.AxisListType
+
+P = 128
+PACK = 4
+D, T, I, Q, J, G, M = 512, 2048, 512, 128, 512, 64, 512
+RUN = I // G
+HALF = I // 2
+
+FLOPS = 2 * D * J * Q + 2 * J * Q * I + 2 * D * Q * I
+
+
+def tile_attend_mixedslots_leaning_pagesums_kernel(
+    tc, query, keys_words, keys_scales, hf, mixer, lean, worth, old, offs, offs2, offs3, out
+):
+    nc = tc.nc
+    with ExitStack() as ctx:
+        sb = ctx.enter_context(tc.tile_pool(name="sb", bufs=1))
+        ps = ctx.enter_context(tc.psum_pool(name="ps", bufs=1))
+
+        list1 = sb.tile([P, I // 16], U16, name="list1")
+        list2 = sb.tile([P, J // 16], U16, name="list2")
+        list3 = sb.tile([P, G // 16], U16, name="list3")
+
+        pool_scales = sb.tile([P, T], U8, name="pool_scales", tag="scales_then_worth", align_bytes=64)
+        nc.vector.memset(pool_scales[:].bitcast(I32), 0)
+
+        nc.sync.dma_start(list2[:], offs2)
+        nc.sync.dma_start(list1[:], offs)
+        for quad in range(4):
+            nc.sync.dma_start(
+                pool_scales[32 * quad : 32 * quad + 4, :].bitcast(I32),
+                keys_scales[0, 4 * quad : 4 * quad + 4, :].bitcast(I32),
+            )
+        q_raw = sb.tile([P, PACK, Q], F32, name="q_raw", tag="query_then_old", align_bytes=64)
+        nc.sync.dma_start(q_raw[:], query.rearrange("(p t) q -> p t q", t=PACK))
+        pool_words = sb.tile([P, T], I32, name="pool_words", align_bytes=64)
+        nc.sync.dma_start(pool_words[:], keys_words[0].rearrange("p c r -> p (c r)").bitcast(I32))
+        mixer_rows = mixer.rearrange("(p t) i -> p t i", t=PACK)
+        m_raw = [sb.tile([P, PACK, HALF], F32, name="m_raw%d" % h) for h in range(2)]
+        for h in range(2):
+            nc.sync.dma_start(m_raw[h][:], mixer_rows[:, :, h * HALF : (h + 1) * HALF])
+        nc.sync.dma_start(list3[:], offs3)
+
+        hf_sb = sb.tile([P, PACK], F32, name="hf_sb")
+        nc.sync.dma_start(hf_sb[:], hf.rearrange("(p t) o -> p (t o)", t=PACK))
+        lean_sb = sb.tile([P, 1], F32, name="lean_sb")
+        nc.sync.dma_start(lean_sb[:], lean)
+
+        warm_in = sb.tile([P, 1], F32, name="warm_in")
+        warm_out = sb.tile([P, 1], F32, name="warm_out")
+        nc.vector.memset(warm_in[:], 0.0)
+        nc.scalar.activation(warm_out[:], warm_in[:], ACT.Exp)
+
+        placed = sb.tile([P, M], F32, name="placed")
+        nc.vector.memset(placed[:], 0.0)
+
+        s2_listed = sb.tile([P, J], U8, name="s2_listed", align_bytes=64)
+        nc.vector.tensor_copy(s2_listed[:], pool_scales[:].indirect(list2[:]))
+        s2 = sb.tile([P, J], U8, name="s2", align_bytes=64)
+        nc.vector.tensor_copy(
+            s2[:].rearrange("p (t s) -> p t s", t=PACK), s2_listed[:].rearrange("p (s t) -> p t s", t=PACK)
+        )
+        s1 = sb.tile([P, I], U8, name="s1", align_bytes=64)
+        nc.vector.tensor_copy(s1[:], pool_scales[:].indirect(list1[:]))
+
+        worth_sb = sb.tile([P, T], F32, name="worth_sb", tag="scales_then_worth", align_bytes=64)
+        nc.sync.dma_start(worth_sb[:], worth)
+
+        q_bf = sb.tile([P, Q, PACK], BF16, name="q_bf", align_bytes=64)
+        nc.scalar.copy(q_bf[:], q_raw[:].rearrange("p t q -> p q t"))
+        q_codes = sb.tile([P, Q], U32, name="q_codes", align_bytes=64)
+        q_scales = sb.tile([P, Q], U8, name="q_scales", align_bytes=64)
+        nc.vector.quantize_mx(q_codes[:].bitcast(FP8X4), q_scales[:], q_bf[:].rearrange("p q t -> p (q t)"))
+
+        old_sb = sb.tile([P, M], F32, name="old_sb", tag="query_then_old", align_bytes=64)
+        nc.sync.dma_start(old_sb[:], old)
+
+        w2 = sb.tile([P, J], U32, name="w2", align_bytes=64)
+        nc.vector.tensor_copy(
+            w2[:].rearrange("p (t s) -> p s t", t=PACK), pool_words[:].bitcast(U32).indirect(list2[:])
+        )
+        w1 = sb.tile([P, I], U32, name="w1", align_bytes=64)
+        nc.vector.tensor_copy(w1[:], pool_words[:].bitcast(U32).indirect(list1[:]))
+
+        a0 = ps.tile([P, PACK, Q], F32, name="a0")
+        for t in range(PACK):
+            cols = slice(t * P, (t + 1) * P)
+            nc.tensor.matmul_mx(
+                out=a0[:, t, :], lhsT=w2[:, cols].bitcast(FP8X4), lhsT_scale=s2[:, cols],
+                rhs=q_codes[:].bitcast(FP8X4), rhs_scale=q_scales[:], start=True, stop=True,
+            )
+        s_ps = ps.tile([P, I], F32, name="s_ps")
+        nc.tensor.matmul_mx(
+            out=s_ps[:], lhsT=q_codes[:].bitcast(FP8X4), lhsT_scale=q_scales[:],
+            rhs=w1[:].bitcast(FP8X4), rhs_scale=s1[:], start=True, stop=False,
+        )
+
+        af_bf = sb.tile([P, Q, PACK], BF16, name="af_bf", tag="af_then_worth", align_bytes=64)
+        nc.vector.tensor_tensor(
+            af_bf[:], a0[:].rearrange("p t q -> p q t"), hf_sb[:].unsqueeze(1).to_broadcast([P, Q, PACK]), ALU.mult
+        )
+
+        m_codes = sb.tile([P, I], U32, name="m_codes", align_bytes=64)
+        m_scales = sb.tile([P, I], U8, name="m_scales", align_bytes=64)
+        for h in range(2):
+            m_bf = sb.tile([P, HALF, PACK], BF16, name="m_bf%d" % h, align_bytes=64)
+            nc.scalar.copy(
+                m_bf[:].rearrange("p (c i) t -> p c t i", i=4), m_raw[h][:].rearrange("p t (c i) -> p c t i", i=4)
+            )
+            cols = slice(h * HALF, (h + 1) * HALF)
+            nc.vector.quantize_mx(
+                m_codes[:, cols].bitcast(FP8X4), m_scales[:, cols], m_bf[:].rearrange("p i t -> p (i t)")
+            )
+
+        af_codes = sb.tile([P, Q], U32, name="af_codes", align_bytes=64)
+        af_scales = sb.tile([P, Q], U8, name="af_scales", align_bytes=64)
+        nc.vector.quantize_mx(af_codes[:].bitcast(FP8X4), af_scales[:], af_bf[:].rearrange("p q t -> p (q t)"))
+        nc.tensor.matmul_mx(
+            out=s_ps[:], lhsT=af_codes[:].bitcast(FP8X4), lhsT_scale=af_scales[:],
+            rhs=m_codes[:].bitcast(FP8X4), rhs_scale=m_scales[:], start=False, stop=True,
+        )
+
+        lean256 = sb.tile([P, 1], F32, name="lean256")
+        nc.vector.tensor_scalar(lean256[:], lean_sb[:], 256.0, None, ALU.mult)
+
+        worth_a = sb.tile([P, HALF], F32, name="worth_a", tag="af_then_worth", align_bytes=64)
+        nc.vector.tensor_copy(worth_a[:], worth_sb[:].indirect(list1[:, 0 : HALF // 16]))
+
+        neg_s = sb.tile([P, I], F32, name="neg_s")
+        neg_max = sb.tile([P, 1], F32, name="neg_max")
+        nc.vector.tensor_scalar(neg_s[:], s_ps[:], -1.0, None, ALU.mult, ALU.min, accum_out=neg_max[:])
+
+        e = sb.tile([P, I], F32, name="e")
+        z = sb.tile([P, 1], F32, name="z")
+        nc.scalar.activation(e[:], s_ps[:], ACT.Exp, bias=neg_max[:], accum_out=z[:])
+
+        shift = sb.tile([P, 1], F32, name="shift")
+        nc.vector.tensor_scalar(shift[:], neg_max[:], lean256[:], 256.0, ALU.mult, ALU.add)
+        worth_b = sb.tile([P, HALF], F32, name="worth_b")
+        nc.vector.tensor_copy(worth_b[:], worth_sb[:].indirect(list1[:, HALF // 16 : I // 16]))
+        leaned = sb.tile([P, I], F32, name="leaned")
+        nc.scalar.activation(leaned[:], s_ps[:], ACT.Identity, bias=shift[:], scale=lean256[:])
+
+        inv_z = sb.tile([P, 1], F32, name="inv_z")
+        nc.vector.reciprocal(inv_z[:], z[:])
+        gap_e = sb.tile([P, I], F32, name="gap_e")
+        gap_sum = sb.tile([P, 1], F32, name="gap_sum")
+        nc.vector.scalar_tensor_tensor(
+            gap_e[:], neg_s[:], neg_max[:], e[:], ALU.subtract, ALU.mult, accum_out=gap_sum[:]
+        )
+        rw = sb.tile([P, I], F32, name="rw")
+        for h, listed in enumerate((worth_a, worth_b)):
+            cols = slice(h * HALF, (h + 1) * HALF)
+            nc.vector.scalar_tensor_tensor(rw[:, cols], e[:, cols], inv_z[:], listed[:], ALU.mult, ALU.mult)
+        lift = sb.tile([P, 1], F32, name="lift")
+        nc.vector.tensor_scalar(lift[:], gap_sum[:], inv_z[:], lean256[:], ALU.mult, ALU.mult)
+        ws = sb.tile([P, I], F32, name="ws")
+        wp = sb.tile([P, G], F32, name="wp")
+        for h in range(2):
+            cols = slice(h * HALF, (h + 1) * HALF)
+            nc.vector.scalar_tensor_tensor(ws[:, cols], leaned[:, cols], lift[:], rw[:, cols], ALU.add, ALU.mult)
+        for h in range(2):
+            cols = slice(h * HALF, (h + 1) * HALF)
+            nc.vector.tensor_reduce(
+                wp[:, h * G // 2 : (h + 1) * G // 2], ws[:, cols].rearrange("p (g r) -> p g r", r=RUN), AXIS.X, ALU.add
+            )
+        nc.vector.tensor_copy(placed[:].indirect(list3[:]), wp[:])
+        for h, queue in enumerate((nc.sync, nc.scalar)):
+            cols = slice(h * M // 2, (h + 1) * M // 2)
+            y = sb.tile([P, M // 2], F32, name="y%d" % h)
+            nc.vector.tensor_tensor(y[:], placed[:, cols], old_sb[:, cols], ALU.add)
+            queue.dma_start(out[:, cols], y[:])

@@ -1,6 +1,7 @@
 from contextlib import ExitStack
 
 import concourse.mybir as mybir
+from concourse.masks import make_identity
 
 F32 = mybir.dt.float32
 BF16 = mybir.dt.bfloat16
@@ -18,6 +19,7 @@ PACK = 4
 D, T, I, Q, J, G, M = 512, 2048, 512, 128, 512, 64, 512
 RUN = I // G
 HALF = I // 2
+MIXER_PIECES = (slice(0, 256), slice(256, 512))
 
 FLOPS = 2 * D * J * Q + 2 * J * Q * I + 2 * D * Q * I
 
@@ -34,30 +36,35 @@ def tile_attend_mixedslots_leaning_pagesums_kernel(
         list2 = sb.tile([P, J // 16], U16, name="list2")
         list3 = sb.tile([P, G // 16], U16, name="list3")
 
-        pool_scales = sb.tile([P, T], U8, name="pool_scales", tag="scales_then_worth", align_bytes=64)
+        pool_scales = sb.tile([P, T], U8, name="pool_scales", align_bytes=64)
         nc.vector.memset(pool_scales[:].bitcast(I32), 0)
 
         nc.sync.dma_start(list2[:], offs2)
         nc.sync.dma_start(list1[:], offs)
+        worth_cols = sb.tile([P, T // P], F32, name="worth_cols", tag="worth_then_query", align_bytes=64)
+        nc.sync.dma_start(worth_cols[:], worth[0:1, :].rearrange("o (p c) -> (o p) c", p=P))
         for quad in range(4):
             nc.sync.dma_start(
                 pool_scales[32 * quad : 32 * quad + 4, :].bitcast(I32),
                 keys_scales[0, 4 * quad : 4 * quad + 4, :].bitcast(I32),
             )
-        q_raw = sb.tile([P, PACK, Q], F32, name="q_raw", tag="query_then_old", align_bytes=64)
-        nc.sync.dma_start(q_raw[:], query.rearrange("(p t) q -> p t q", t=PACK))
         pool_words = sb.tile([P, T], I32, name="pool_words", align_bytes=64)
         nc.sync.dma_start(pool_words[:], keys_words[0].rearrange("p c r -> p (c r)").bitcast(I32))
-        mixer_rows = mixer.rearrange("(p t) i -> p t i", t=PACK)
-        m_raw = [sb.tile([P, PACK, HALF], F32, name="m_raw%d" % h) for h in range(2)]
-        for h in range(2):
-            nc.sync.dma_start(m_raw[h][:], mixer_rows[:, :, h * HALF : (h + 1) * HALF])
-        nc.sync.dma_start(list3[:], offs3)
-
+        q_raw = sb.tile([P, PACK, Q], F32, name="q_raw", tag="query_then_words", align_bytes=64)
+        nc.sync.dma_start(q_raw[:], query.rearrange("(p t) q -> p t q", t=PACK))
         hf_sb = sb.tile([P, PACK], F32, name="hf_sb")
         nc.sync.dma_start(hf_sb[:], hf.rearrange("(p t) o -> p (t o)", t=PACK))
+        mixer_rows = mixer.rearrange("(p t) i -> p t i", t=PACK)
+        m_raw = []
+        for n, cols in enumerate(MIXER_PIECES):
+            piece = sb.tile([P, PACK, cols.stop - cols.start], F32, name="m_raw%d" % n, tag="mixer%d" % n, align_bytes=64)
+            nc.sync.dma_start(piece[:], mixer_rows[:, :, cols])
+            m_raw.append(piece)
         lean_sb = sb.tile([P, 1], F32, name="lean_sb")
         nc.sync.dma_start(lean_sb[:], lean)
+        nc.sync.dma_start(list3[:], offs3)
+        old_sb = sb.tile([P, M], F32, name="old_sb")
+        nc.sync.dma_start(old_sb[:], old)
 
         warm_in = sb.tile([P, 1], F32, name="warm_in")
         warm_out = sb.tile([P, 1], F32, name="warm_out")
@@ -67,32 +74,38 @@ def tile_attend_mixedslots_leaning_pagesums_kernel(
         placed = sb.tile([P, M], F32, name="placed")
         nc.vector.memset(placed[:], 0.0)
 
+        identity = sb.tile([P, P], F32, name="identity", tag="mixer_bf", align_bytes=64)
+        make_identity(nc, identity[:])
+        worth_sb = sb.tile([P, T], F32, name="worth_sb")
+        worth_by_bank = worth_sb[:].rearrange("m (p b c) -> m b p c", b=4, c=4)
+        for b in range(4):
+            spread = ps.tile([P, 4, P], F32, name="spread%d" % b)
+            for c in range(4):
+                col = 4 * b + c
+                nc.tensor.transpose(spread[:, c, :], worth_cols[:, col : col + 1].to_broadcast([P, P]), identity[:])
+            nc.scalar.copy(worth_by_bank[:, b], spread[:].rearrange("m c p -> m p c"))
+
         s2_listed = sb.tile([P, J], U8, name="s2_listed", align_bytes=64)
         nc.vector.tensor_copy(s2_listed[:], pool_scales[:].indirect(list2[:]))
+        s1 = sb.tile([P, I], U8, name="s1", align_bytes=64)
+        nc.vector.tensor_copy(s1[:], pool_scales[:].indirect(list1[:]))
         s2 = sb.tile([P, J], U8, name="s2", align_bytes=64)
         nc.vector.tensor_copy(
             s2[:].rearrange("p (t s) -> p t s", t=PACK), s2_listed[:].rearrange("p (s t) -> p t s", t=PACK)
         )
-        s1 = sb.tile([P, I], U8, name="s1", align_bytes=64)
-        nc.vector.tensor_copy(s1[:], pool_scales[:].indirect(list1[:]))
 
-        worth_sb = sb.tile([P, T], F32, name="worth_sb", tag="scales_then_worth", align_bytes=64)
-        nc.sync.dma_start(worth_sb[:], worth)
-
-        q_bf = sb.tile([P, Q, PACK], BF16, name="q_bf", align_bytes=64)
+        q_bf = sb.tile([P, Q, PACK], BF16, name="q_bf", tag="worth_then_query", align_bytes=64)
         nc.scalar.copy(q_bf[:], q_raw[:].rearrange("p t q -> p q t"))
         q_codes = sb.tile([P, Q], U32, name="q_codes", align_bytes=64)
         q_scales = sb.tile([P, Q], U8, name="q_scales", align_bytes=64)
         nc.vector.quantize_mx(q_codes[:].bitcast(FP8X4), q_scales[:], q_bf[:].rearrange("p q t -> p (q t)"))
 
-        old_sb = sb.tile([P, M], F32, name="old_sb", tag="query_then_old", align_bytes=64)
-        nc.sync.dma_start(old_sb[:], old)
-
         w2 = sb.tile([P, J], U32, name="w2", align_bytes=64)
         nc.vector.tensor_copy(
             w2[:].rearrange("p (t s) -> p s t", t=PACK), pool_words[:].bitcast(U32).indirect(list2[:])
         )
-        w1 = sb.tile([P, I], U32, name="w1", align_bytes=64)
+        halves = [slice(h * HALF, (h + 1) * HALF) for h in range(2)]
+        w1 = sb.tile([P, I], U32, name="w1", tag="query_then_words", align_bytes=64)
         nc.vector.tensor_copy(w1[:], pool_words[:].bitcast(U32).indirect(list1[:]))
 
         a0 = ps.tile([P, PACK, Q], F32, name="a0")
@@ -108,35 +121,35 @@ def tile_attend_mixedslots_leaning_pagesums_kernel(
             rhs=w1[:].bitcast(FP8X4), rhs_scale=s1[:], start=True, stop=False,
         )
 
-        af_bf = sb.tile([P, Q, PACK], BF16, name="af_bf", tag="af_then_worth", align_bytes=64)
+        af_bf = sb.tile([P, Q, PACK], BF16, name="af_bf", align_bytes=64)
         nc.vector.tensor_tensor(
             af_bf[:], a0[:].rearrange("p t q -> p q t"), hf_sb[:].unsqueeze(1).to_broadcast([P, Q, PACK]), ALU.mult
         )
 
-        m_codes = sb.tile([P, I], U32, name="m_codes", align_bytes=64)
+        m_bf = sb.tile([P, I, PACK], BF16, name="m_bf", tag="mixer_bf", align_bytes=64)
+        m_codes = sb.tile([P, I], U32, name="m_codes", tag="mixer_codes", align_bytes=64)
         m_scales = sb.tile([P, I], U8, name="m_scales", align_bytes=64)
-        for h in range(2):
-            m_bf = sb.tile([P, HALF, PACK], BF16, name="m_bf%d" % h, align_bytes=64)
+        for piece, cols in zip(m_raw, MIXER_PIECES):
             nc.scalar.copy(
-                m_bf[:].rearrange("p (c i) t -> p c t i", i=4), m_raw[h][:].rearrange("p t (c i) -> p c t i", i=4)
-            )
-            cols = slice(h * HALF, (h + 1) * HALF)
-            nc.vector.quantize_mx(
-                m_codes[:, cols].bitcast(FP8X4), m_scales[:, cols], m_bf[:].rearrange("p i t -> p (i t)")
+                m_bf[:, cols, :].rearrange("p (c i) t -> p c t i", i=4), piece[:].rearrange("p t (c i) -> p c t i", i=4)
             )
 
-        af_codes = sb.tile([P, Q], U32, name="af_codes", align_bytes=64)
+        def quantize_mixer(h):
+            nc.vector.quantize_mx(
+                m_codes[:, halves[h]].bitcast(FP8X4), m_scales[:, halves[h]], m_bf[:, halves[h], :].rearrange("p i t -> p (i t)")
+            )
+
+        quantize_mixer(0)
+        af_codes = sb.tile([P, Q], U32, name="af_codes", tag="mixer0", align_bytes=64)
         af_scales = sb.tile([P, Q], U8, name="af_scales", align_bytes=64)
         nc.vector.quantize_mx(af_codes[:].bitcast(FP8X4), af_scales[:], af_bf[:].rearrange("p q t -> p (q t)"))
+        quantize_mixer(1)
         nc.tensor.matmul_mx(
             out=s_ps[:], lhsT=af_codes[:].bitcast(FP8X4), lhsT_scale=af_scales[:],
             rhs=m_codes[:].bitcast(FP8X4), rhs_scale=m_scales[:], start=False, stop=True,
         )
 
-        lean256 = sb.tile([P, 1], F32, name="lean256")
-        nc.vector.tensor_scalar(lean256[:], lean_sb[:], 256.0, None, ALU.mult)
-
-        worth_a = sb.tile([P, HALF], F32, name="worth_a", tag="af_then_worth", align_bytes=64)
+        worth_a = sb.tile([P, HALF], F32, name="worth_a", tag="mixer_bf", align_bytes=64)
         nc.vector.tensor_copy(worth_a[:], worth_sb[:].indirect(list1[:, 0 : HALF // 16]))
 
         neg_s = sb.tile([P, I], F32, name="neg_s")
@@ -147,12 +160,12 @@ def tile_attend_mixedslots_leaning_pagesums_kernel(
         z = sb.tile([P, 1], F32, name="z")
         nc.scalar.activation(e[:], s_ps[:], ACT.Exp, bias=neg_max[:], accum_out=z[:])
 
-        shift = sb.tile([P, 1], F32, name="shift")
-        nc.vector.tensor_scalar(shift[:], neg_max[:], lean256[:], 256.0, ALU.mult, ALU.add)
-        worth_b = sb.tile([P, HALF], F32, name="worth_b")
+        worth_b = sb.tile([P, HALF], F32, name="worth_b", tag="mixer_codes", align_bytes=64)
         nc.vector.tensor_copy(worth_b[:], worth_sb[:].indirect(list1[:, HALF // 16 : I // 16]))
+        shift = sb.tile([P, 1], F32, name="shift")
+        nc.vector.tensor_scalar(shift[:], neg_max[:], lean_sb[:], 1.0, ALU.mult, ALU.add)
         leaned = sb.tile([P, I], F32, name="leaned")
-        nc.scalar.activation(leaned[:], s_ps[:], ACT.Identity, bias=shift[:], scale=lean256[:])
+        nc.scalar.activation(leaned[:], s_ps[:], ACT.Identity, bias=shift[:], scale=lean_sb[:])
 
         inv_z = sb.tile([P, 1], F32, name="inv_z")
         nc.vector.reciprocal(inv_z[:], z[:])
@@ -161,25 +174,22 @@ def tile_attend_mixedslots_leaning_pagesums_kernel(
         nc.vector.scalar_tensor_tensor(
             gap_e[:], neg_s[:], neg_max[:], e[:], ALU.subtract, ALU.mult, accum_out=gap_sum[:]
         )
-        rw = sb.tile([P, I], F32, name="rw")
-        for h, listed in enumerate((worth_a, worth_b)):
-            cols = slice(h * HALF, (h + 1) * HALF)
-            nc.vector.scalar_tensor_tensor(rw[:, cols], e[:, cols], inv_z[:], listed[:], ALU.mult, ALU.mult)
+        rw = [sb.tile([P, HALF], F32, name="rw%d" % h) for h in range(2)]
         lift = sb.tile([P, 1], F32, name="lift")
-        nc.vector.tensor_scalar(lift[:], gap_sum[:], inv_z[:], lean256[:], ALU.mult, ALU.mult)
-        ws = sb.tile([P, I], F32, name="ws")
-        wp = sb.tile([P, G], F32, name="wp")
+        nc.vector.scalar_tensor_tensor(rw[0][:], e[:, halves[0]], inv_z[:], worth_a[:], ALU.mult, ALU.mult)
+        nc.vector.tensor_scalar(lift[:], gap_sum[:], inv_z[:], lean_sb[:], ALU.mult, ALU.mult)
+        nc.vector.scalar_tensor_tensor(rw[1][:], e[:, halves[1]], inv_z[:], worth_b[:], ALU.mult, ALU.mult)
+        ws = [sb.tile([P, HALF], F32, name="ws%d" % h) for h in range(2)]
         for h in range(2):
-            cols = slice(h * HALF, (h + 1) * HALF)
-            nc.vector.scalar_tensor_tensor(ws[:, cols], leaned[:, cols], lift[:], rw[:, cols], ALU.add, ALU.mult)
+            nc.vector.scalar_tensor_tensor(ws[h][:], leaned[:, halves[h]], lift[:], rw[h][:], ALU.add, ALU.mult)
+        run_sums = sb.tile([P, G], F32, name="run_sums")
         for h in range(2):
-            cols = slice(h * HALF, (h + 1) * HALF)
             nc.vector.tensor_reduce(
-                wp[:, h * G // 2 : (h + 1) * G // 2], ws[:, cols].rearrange("p (g r) -> p g r", r=RUN), AXIS.X, ALU.add
+                run_sums[:, h * G // 2 : (h + 1) * G // 2], ws[h][:].rearrange("p (g r) -> p g r", r=RUN), AXIS.X, ALU.add
             )
-        nc.vector.tensor_copy(placed[:].indirect(list3[:]), wp[:])
+        nc.vector.tensor_copy(placed[:].indirect(list3[:]), run_sums[:])
         for h, queue in enumerate((nc.sync, nc.scalar)):
             cols = slice(h * M // 2, (h + 1) * M // 2)
             y = sb.tile([P, M // 2], F32, name="y%d" % h)
-            nc.vector.tensor_tensor(y[:], placed[:, cols], old_sb[:, cols], ALU.add)
+            nc.vector.scalar_tensor_tensor(y[:], placed[:, cols], 256.0, old_sb[:, cols], ALU.mult, ALU.add)
             queue.dma_start(out[:, cols], y[:])

from contextlib import ExitStack

import concourse.mybir as mybir
from concourse.masks import make_identity

F32 = mybir.dt.float32
BF16 = mybir.dt.bfloat16
I32 = mybir.dt.int32
U32 = mybir.dt.uint32
U16 = mybir.dt.uint16
U8 = mybir.dt.uint8
FP8X4 = mybir.dt.float8_e4m3fn_x4
ALU = mybir.AluOpType
ACT = mybir.ActivationFunctionType
AXIS = mybir.AxisListType

P = 128
PACK = 4
D, T, I, Q, J, G, M = 512, 2048, 512, 128, 512, 64, 512
RUN = I // G
HALF = I // 2
MIXER_PIECES = (slice(0, 256), slice(256, 512))

FLOPS = 2 * D * J * Q + 2 * J * Q * I + 2 * D * Q * I


def tile_attend_mixedslots_leaning_pagesums_kernel(
    tc, query, keys_words, keys_scales, hf, mixer, lean, worth, old, offs, offs2, offs3, out
):
    nc = tc.nc
    with ExitStack() as ctx:
        sb = ctx.enter_context(tc.tile_pool(name="sb", bufs=1))
        ps = ctx.enter_context(tc.psum_pool(name="ps", bufs=1))

        list1 = sb.tile([P, I // 16], U16, name="list1")
        list2 = sb.tile([P, J // 16], U16, name="list2")
        list3 = sb.tile([P, G // 16], U16, name="list3")

        pool_scales = sb.tile([P, T], U8, name="pool_scales", align_bytes=64)
        nc.vector.memset(pool_scales[:].bitcast(I32), 0)

        nc.sync.dma_start(list2[:], offs2)
        nc.sync.dma_start(list1[:], offs)
        worth_cols = sb.tile([P, T // P], F32, name="worth_cols", tag="worth_then_query", align_bytes=64)
        nc.sync.dma_start(worth_cols[:], worth[0:1, :].rearrange("o (p c) -> (o p) c", p=P))
        for quad in range(4):
            nc.sync.dma_start(
                pool_scales[32 * quad : 32 * quad + 4, :].bitcast(I32),
                keys_scales[0, 4 * quad : 4 * quad + 4, :].bitcast(I32),
            )
        pool_words = sb.tile([P, T], I32, name="pool_words", align_bytes=64)
        nc.sync.dma_start(pool_words[:], keys_words[0].rearrange("p c r -> p (c r)").bitcast(I32))
        q_raw = sb.tile([P, PACK, Q], F32, name="q_raw", tag="query_then_words", align_bytes=64)
        nc.sync.dma_start(q_raw[:], query.rearrange("(p t) q -> p t q", t=PACK))
        hf_sb = sb.tile([P, PACK], F32, name="hf_sb")
        nc.sync.dma_start(hf_sb[:], hf.rearrange("(p t) o -> p (t o)", t=PACK))
        mixer_rows = mixer.rearrange("(p t) i -> p t i", t=PACK)
        m_raw = []
        for n, cols in enumerate(MIXER_PIECES):
            piece = sb.tile([P, PACK, cols.stop - cols.start], F32, name="m_raw%d" % n, tag="mixer%d" % n, align_bytes=64)
            nc.sync.dma_start(piece[:], mixer_rows[:, :, cols])
            m_raw.append(piece)
        lean_sb = sb.tile([P, 1], F32, name="lean_sb")
        nc.sync.dma_start(lean_sb[:], lean)
        nc.sync.dma_start(list3[:], offs3)
        old_sb = sb.tile([P, M], F32, name="old_sb")
        nc.sync.dma_start(old_sb[:], old)

        warm_in = sb.tile([P, 1], F32, name="warm_in")
        warm_out = sb.tile([P, 1], F32, name="warm_out")
        nc.vector.memset(warm_in[:], 0.0)
        nc.scalar.activation(warm_out[:], warm_in[:], ACT.Exp)

        placed = sb.tile([P, M], F32, name="placed")
        nc.vector.memset(placed[:], 0.0)

        identity = sb.tile([P, P], F32, name="identity", tag="mixer_bf", align_bytes=64)
        make_identity(nc, identity[:])
        worth_sb = sb.tile([P, T], F32, name="worth_sb")
        worth_by_bank = worth_sb[:].rearrange("m (p b c) -> m b p c", b=4, c=4)
        for b in range(4):
            spread = ps.tile([P, 4, P], F32, name="spread%d" % b)
            for c in range(4):
                col = 4 * b + c
                nc.tensor.transpose(spread[:, c, :], worth_cols[:, col : col + 1].to_broadcast([P, P]), identity[:])
            nc.scalar.copy(worth_by_bank[:, b], spread[:].rearrange("m c p -> m p c"))

        s2_listed = sb.tile([P, J], U8, name="s2_listed", align_bytes=64)
        nc.vector.tensor_copy(s2_listed[:], pool_scales[:].indirect(list2[:]))
        s1 = sb.tile([P, I], U8, name="s1", align_bytes=64)
        nc.vector.tensor_copy(s1[:], pool_scales[:].indirect(list1[:]))
        s2 = sb.tile([P, J], U8, name="s2", align_bytes=64)
        nc.vector.tensor_copy(
            s2[:].rearrange("p (t s) -> p t s", t=PACK), s2_listed[:].rearrange("p (s t) -> p t s", t=PACK)
        )

        q_bf = sb.tile([P, Q, PACK], BF16, name="q_bf", tag="worth_then_query", align_bytes=64)
        nc.scalar.copy(q_bf[:], q_raw[:].rearrange("p t q -> p q t"))
        q_codes = sb.tile([P, Q], U32, name="q_codes", align_bytes=64)
        q_scales = sb.tile([P, Q], U8, name="q_scales", align_bytes=64)
        nc.vector.quantize_mx(q_codes[:].bitcast(FP8X4), q_scales[:], q_bf[:].rearrange("p q t -> p (q t)"))

        w2 = sb.tile([P, J], U32, name="w2", align_bytes=64)
        nc.vector.tensor_copy(
            w2[:].rearrange("p (t s) -> p s t", t=PACK), pool_words[:].bitcast(U32).indirect(list2[:])
        )
        halves = [slice(h * HALF, (h + 1) * HALF) for h in range(2)]
        w1 = sb.tile([P, I], U32, name="w1", tag="query_then_words", align_bytes=64)
        nc.vector.tensor_copy(w1[:], pool_words[:].bitcast(U32).indirect(list1[:]))

        a0 = ps.tile([P, PACK, Q], F32, name="a0")
        for t in range(PACK):
            cols = slice(t * P, (t + 1) * P)
            nc.tensor.matmul_mx(
                out=a0[:, t, :], lhsT=w2[:, cols].bitcast(FP8X4), lhsT_scale=s2[:, cols],
                rhs=q_codes[:].bitcast(FP8X4), rhs_scale=q_scales[:], start=True, stop=True,
            )
        s_ps = ps.tile([P, I], F32, name="s_ps")
        nc.tensor.matmul_mx(
            out=s_ps[:], lhsT=q_codes[:].bitcast(FP8X4), lhsT_scale=q_scales[:],
            rhs=w1[:].bitcast(FP8X4), rhs_scale=s1[:], start=True, stop=False,
        )

        af_bf = sb.tile([P, Q, PACK], BF16, name="af_bf", align_bytes=64)
        nc.vector.tensor_tensor(
            af_bf[:], a0[:].rearrange("p t q -> p q t"), hf_sb[:].unsqueeze(1).to_broadcast([P, Q, PACK]), ALU.mult
        )

        m_bf = sb.tile([P, I, PACK], BF16, name="m_bf", tag="mixer_bf", align_bytes=64)
        m_codes = sb.tile([P, I], U32, name="m_codes", tag="mixer_codes", align_bytes=64)
        m_scales = sb.tile([P, I], U8, name="m_scales", align_bytes=64)
        for piece, cols in zip(m_raw, MIXER_PIECES):
            nc.scalar.copy(
                m_bf[:, cols, :].rearrange("p (c i) t -> p c t i", i=4), piece[:].rearrange("p t (c i) -> p c t i", i=4)
            )

        def quantize_mixer(h):
            nc.vector.quantize_mx(
                m_codes[:, halves[h]].bitcast(FP8X4), m_scales[:, halves[h]], m_bf[:, halves[h], :].rearrange("p i t -> p (i t)")
            )

        quantize_mixer(0)
        af_codes = sb.tile([P, Q], U32, name="af_codes", tag="mixer0", align_bytes=64)
        af_scales = sb.tile([P, Q], U8, name="af_scales", align_bytes=64)
        nc.vector.quantize_mx(af_codes[:].bitcast(FP8X4), af_scales[:], af_bf[:].rearrange("p q t -> p (q t)"))
        quantize_mixer(1)
        nc.tensor.matmul_mx(
            out=s_ps[:], lhsT=af_codes[:].bitcast(FP8X4), lhsT_scale=af_scales[:],
            rhs=m_codes[:].bitcast(FP8X4), rhs_scale=m_scales[:], start=False, stop=True,
        )

        worth_a = sb.tile([P, HALF], F32, name="worth_a", tag="mixer_bf", align_bytes=64)
        nc.vector.tensor_copy(worth_a[:], worth_sb[:].indirect(list1[:, 0 : HALF // 16]))

        neg_s = sb.tile([P, I], F32, name="neg_s")
        neg_max = sb.tile([P, 1], F32, name="neg_max")
        nc.vector.tensor_scalar(neg_s[:], s_ps[:], -1.0, None, ALU.mult, ALU.min, accum_out=neg_max[:])

        e = sb.tile([P, I], F32, name="e")
        z = sb.tile([P, 1], F32, name="z")
        nc.scalar.activation(e[:], s_ps[:], ACT.Exp, bias=neg_max[:], accum_out=z[:])

        worth_b = sb.tile([P, HALF], F32, name="worth_b", tag="mixer_codes", align_bytes=64)
        nc.vector.tensor_copy(worth_b[:], worth_sb[:].indirect(list1[:, HALF // 16 : I // 16]))
        shift = sb.tile([P, 1], F32, name="shift")
        nc.vector.tensor_scalar(shift[:], neg_max[:], lean_sb[:], 1.0, ALU.mult, ALU.add)
        leaned = sb.tile([P, I], F32, name="leaned")
        nc.scalar.activation(leaned[:], s_ps[:], ACT.Identity, bias=shift[:], scale=lean_sb[:])

        inv_z = sb.tile([P, 1], F32, name="inv_z")
        nc.vector.reciprocal(inv_z[:], z[:])
        gap_e = sb.tile([P, I], F32, name="gap_e")
        gap_sum = sb.tile([P, 1], F32, name="gap_sum")
        nc.vector.scalar_tensor_tensor(
            gap_e[:], neg_s[:], neg_max[:], e[:], ALU.subtract, ALU.mult, accum_out=gap_sum[:]
        )
        rw = [sb.tile([P, HALF], F32, name="rw%d" % h) for h in range(2)]
        lift = sb.tile([P, 1], F32, name="lift")
        nc.vector.scalar_tensor_tensor(rw[0][:], e[:, halves[0]], inv_z[:], worth_a[:], ALU.mult, ALU.mult)
        nc.vector.tensor_scalar(lift[:], gap_sum[:], inv_z[:], lean_sb[:], ALU.mult, ALU.mult)
        nc.vector.scalar_tensor_tensor(rw[1][:], e[:, halves[1]], inv_z[:], worth_b[:], ALU.mult, ALU.mult)
        ws = [sb.tile([P, HALF], F32, name="ws%d" % h) for h in range(2)]
        for h in range(2):
            nc.vector.scalar_tensor_tensor(ws[h][:], leaned[:, halves[h]], lift[:], rw[h][:], ALU.add, ALU.mult)
        run_sums = sb.tile([P, G], F32, name="run_sums")
        for h in range(2):
            nc.vector.tensor_reduce(
                run_sums[:, h * G // 2 : (h + 1) * G // 2], ws[h][:].rearrange("p (g r) -> p g r", r=RUN), AXIS.X, ALU.add
            )
        nc.vector.tensor_copy(placed[:].indirect(list3[:]), run_sums[:])
        for h, queue in enumerate((nc.sync, nc.scalar)):
            cols = slice(h * M // 2, (h + 1) * M // 2)
            y = sb.tile([P, M // 2], F32, name="y%d" % h)
            nc.vector.scalar_tensor_tensor(y[:], placed[:, cols], 256.0, old_sb[:, cols], ALU.mult, ALU.add)
            queue.dma_start(out[:, cols], y[:])
